import numpy as np
import ml_dtypes


def mxq(x, axis, fmt="e4m3"):
    dtype, down = {"e4m3": (ml_dtypes.float8_e4m3fn, 7), "e5m2": (ml_dtypes.float8_e5m2, 14)}[fmt]
    v = np.moveaxis(np.asarray(x, np.float32).astype(ml_dtypes.bfloat16).astype(np.float64), axis, -1)
    blocks = v.reshape(v.shape[:-1] + (-1, 32))
    amax = np.abs(blocks).max(-1, keepdims=True)
    byte = np.maximum(np.where(amax > 0, np.frexp(amax)[1] - 1 + 127, 0) - down, 1)
    scale = np.exp2(byte - 127.0)
    codes = (blocks / scale).astype(np.float32).astype(dtype).astype(np.float64)
    return np.moveaxis((codes * scale).reshape(v.shape), -1, axis)


WIDE = False


def mx_kscale(k):
    if not WIDE:
        return np.ones(k)
    levels = np.array([10, -10, 5, -5, 0])
    if k % 512:
        return np.exp2(np.random.permutation(np.resize(levels, k // 32))).repeat(32)
    a = np.empty((k // 512, 16))
    for p in range(k // 512):
        a[p, :8] = np.random.permutation(np.resize(levels, 8))
        for g in range(8):
            far = levels[np.abs(levels - a[p, g]) >= 10]
            a[p, g + 8] = far[np.random.randint(len(far))]
    return np.exp2(a.ravel()).repeat(32)


def f64(x):
    return np.asarray(x).astype(np.float64)


E2M1 = np.array([0.0, 0.5, 1.0, 1.5, 2.0, 3.0, 4.0, 6.0, -0.0, -0.5, -1.0, -1.5, -2.0, -3.0, -4.0, -6.0])


def pack_weight(w, fmt):
    k, n = w.shape
    w = f64(np.asarray(w, np.float32).astype(ml_dtypes.bfloat16)).reshape(k // 32, 32, n)
    amax = np.abs(w).max(1)
    if fmt == "e4m3":
        byte = np.frexp(amax)[1] - 1 + 127 - 7
    else:
        mant, ex = np.frexp(amax / 6.0)
        byte = np.where(mant > 0.5, ex, ex - 1) + 127
    byte = np.clip(np.where(amax > 0, byte, 1), 1, 254)
    scaled = (w * np.exp2(127.0 - byte)[:, None, :]).reshape(k, n).astype(np.float32)
    by_word = np.ascontiguousarray(scaled.reshape(k // 512, 128, 4, n).transpose(0, 1, 3, 2))
    if fmt == "e4m3":
        words = by_word.astype(ml_dtypes.float8_e4m3fn).view(np.uint8)
    else:
        c = by_word.astype(ml_dtypes.float4_e2m1fn).view(np.uint8) & 0xF
        words = (c[..., 0::2] | (c[..., 1::2] << 4)).reshape(k // 512, 128, 2 * n)
    return np.ascontiguousarray(words), np.ascontiguousarray(byte.astype(np.uint8).reshape(k // 512, 16, n))


def unpack_weight(words, scales, fmt):
    g, _, n = scales.shape
    words = np.ascontiguousarray(words).reshape(g, 128, n, -1)
    if fmt == "e4m3":
        vals = words.view(ml_dtypes.float8_e4m3fn).astype(np.float64)
    else:
        nib = np.empty((g, 128, n, 4), np.uint8)
        nib[..., 0::2] = words & 0xF
        nib[..., 1::2] = words >> 4
        vals = E2M1[nib]
    vals = vals * np.repeat(np.exp2(scales.astype(np.float64) - 127.0), 8, axis=1)[..., None]
    return vals.transpose(0, 1, 3, 2).reshape(g * 512, n)


def silu(v):
    return v / (1.0 + np.exp(-np.maximum(v, -700.0)))


K, M, T = 2048, 512, 512


def setup_inputs():
    n = np.random.standard_normal
    s = mx_kscale(K)[:, None]
    p_w4 = pack_weight(n((K, M)) / np.sqrt(K) / s, "e2m1")
    p_w8 = pack_weight(n((K, M)) / np.sqrt(K) / s, "e4m3")
    return {
        "x": (n((K, T)) * s).astype(np.float32),
        "w4_words": p_w4[0],
        "w4_scales": p_w4[1],
        "w8_words": p_w8[0],
        "w8_scales": p_w8[1],
        "b": (0.3 * n(512)).astype(np.float32),
    }


def reference(x, w4_words, w4_scales, w8_words, w8_scales, b):
    xa_, xb_ = mxq(np.maximum(f64(x), 0.0), 0, "e4m3"), mxq(np.maximum(-f64(x), 0.0), 0, "e4m3")
    w4_ = unpack_weight(w4_words, w4_scales, "e2m1")
    w8_ = unpack_weight(w8_words, w8_scales, "e4m3")
    y = xa_.T @ w4_ + xb_.T @ w8_
    return silu(y + f64(b)[None, :])

@@ -1,0 +1,200 @@
+from contextlib import ExitStack
+
+import concourse.mybir as mybir
+from concourse.masks import make_identity
+
+K, N, T = 2048, 512, 512
+FLOPS = 2 * 2 * K * N * T
+
+F32 = mybir.dt.float32
+BF16 = mybir.dt.bfloat16
+I32 = mybir.dt.int32
+U32 = mybir.dt.uint32
+U8 = mybir.dt.uint8
+FP8X4 = mybir.dt.float8_e4m3fn_x4
+FP4X4 = mybir.dt.float4_e2m1fn_x4
+ACT = mybir.ActivationFunctionType
+ALU = mybir.AluOpType
+
+P = 128
+PACK = 4
+K_PASS = P * PACK
+PASSES = K // K_PASS
+T_TILE = 128
+TILES = T // T_TILE
+
+
+def tile_mix_feat_tm_crelu_silu_kernel(tc, x, w4_words, w4_scales, w8_words, w8_scales, b, out):
+    nc = tc.nc
+    last = PASSES - 1
+    chunks = [(g, t0, 256) for g in range(last) for t0 in range(0, T, 256)]
+    chunks = chunks + [(last, t0, T_TILE) for t0 in range(0, T, T_TILE)]
+
+    with ExitStack() as ctx:
+        keep = ctx.enter_context(tc.tile_pool(name="keep", bufs=1))
+        psum = ctx.enter_context(tc.psum_pool(name="psum", bufs=1))
+        ctx.enter_context(tc.manual_schedule())
+
+        def sb(name, shape, dtype):
+            return keep.tile(shape, dtype, name=name, align_bytes=64)
+
+        raw = [sb("raw%d" % c, [P, PACK, w], F32) for c, (g, t0, w) in enumerate(chunks)]
+        xa = [sb("xa%d" % c, [P, w, PACK], BF16) for c, (g, t0, w) in enumerate(chunks)]
+        xb = [sb("xb%d" % c, [P, w, PACK], BF16) for c, (g, t0, w) in enumerate(chunks)]
+        xa_codes = [sb("xac%d" % c, [P, w], U32) for c, (g, t0, w) in enumerate(chunks)]
+        xb_codes = [sb("xbc%d" % c, [P, w], U32) for c, (g, t0, w) in enumerate(chunks)]
+        xa_scales = [sb("xas%d" % c, [P, w], U8) for c, (g, t0, w) in enumerate(chunks)]
+        xb_scales = [sb("xbs%d" % c, [P, w], U8) for c, (g, t0, w) in enumerate(chunks)]
+        w4 = [sb("w4_%d" % h, [P, 2, 2 * N], U8) for h in range(PASSES // 2)]
+        w8 = [sb("w8_%d" % g, [P, N], U32) for g in range(PASSES)]
+        w4_plane = sb("w4_plane", [P, PASSES, N], U8)
+        w8_plane = sb("w8_plane", [P, N], U8)
+        ident = sb("ident", [P, P], F32)
+        b_cols = sb("b_cols", [P, PACK], F32)
+        bias = sb("bias", [P, N], F32)
+        zero_in = sb("zero_in", [P, 1], F32)
+        zero = sb("zero", [P, 1], F32)
+        acc = [psum.tile([P, N], F32, name="acc%d" % i) for i in range(TILES)]
+        bias_ps = psum.tile([P, PACK, P], F32, name="bias_ps")
+
+        w4s = w4_scales.bitcast(I32)
+        w8s = w8_scales.bitcast(I32)
+
+        def load_x(c):
+            g, t0, w = chunks[c]
+            rows = x[g * K_PASS : (g + 1) * K_PASS, t0 : t0 + w]
+            nc.sync.dma_start(out=raw[c][:], in_=rows.rearrange("(p j) t -> p j t", j=PACK))
+
+        def load_w4(h):
+            nc.sync.dma_start(
+                out=w4[h][:].bitcast(I32),
+                in_=w4_words[2 * h : 2 * h + 2].bitcast(I32).rearrange("a p c -> p a c"),
+            )
+
+        def load_w8(g):
+            nc.sync.dma_start(
+                out=w8[g][:].bitcast(I32),
+                in_=w8_words[g].rearrange("p n i -> p (n i)").bitcast(I32),
+            )
+
+        def views(c, dst):
+            return (
+                dst[c][:].rearrange("p (c i) j -> p c j i", i=4),
+                raw[c][:].rearrange("p j (c i) -> p c j i", i=4),
+            )
+
+        def relu_a(c):
+            dst, src = views(c, xa)
+            nc.vector.tensor_scalar(out=dst, in0=src, scalar1=0.0, scalar2=None, op0=ALU.max)
+
+        def relu_b(c):
+            dst, src = views(c, xb)
+            nc.scalar.activation(out=dst, in_=src, func=ACT.Relu, bias=zero[:], scale=-1.0)
+
+        def quantize(values, codes, scales):
+            nc.vector.quantize_mx(
+                out=codes[:].bitcast(FP8X4), scales=scales[:], in_=values[:].rearrange("p t j -> p (t j)")
+            )
+
+        def mm_a(c):
+            g, t0, w = chunks[c]
+            for s in range(0, w, T_TILE):
+                nc.tensor.matmul_mx(
+                    out=acc[(t0 + s) // T_TILE][:],
+                    lhsT=xa_codes[c][:, s : s + T_TILE].bitcast(FP8X4),
+                    lhsT_scale=xa_scales[c][:, s : s + T_TILE],
+                    rhs=w4[g // 2][:, g % 2, :].bitcast(FP4X4),
+                    rhs_scale=w4_plane[:, g, :],
+                    start=(g == 0),
+                    stop=False,
+                )
+
+        def mm_b(c):
+            g, t0, w = chunks[c]
+            for s in range(0, w, T_TILE):
+                nc.tensor.matmul_mx(
+                    out=acc[(t0 + s) // T_TILE][:],
+                    lhsT=xb_codes[c][:, s : s + T_TILE].bitcast(FP8X4),
+                    lhsT_scale=xb_scales[c][:, s : s + T_TILE],
+                    rhs=w8[g][:].bitcast(FP8X4),
+                    rhs_scale=w8_plane[PACK * g :, :],
+                    start=False,
+                    stop=(g == last),
+                )
+
+        nc.vector.memset(w4_plane[:].bitcast(I32), 0)
+        nc.vector.memset(w8_plane[:].bitcast(I32), 0)
+        nc.vector.memset(zero_in[:], 0.0)
+        nc.scalar.activation(out=zero[:], in_=zero_in[:], func=ACT.Silu)
+        make_identity(nc, ident[:])
+
+        load_x(0)
+        for r in range(4):
+            nc.sync.dma_start(
+                out=w4_plane[:].bitcast(I32)[r:P:32, :, :],
+                in_=w4s[:, r:16:4, :].rearrange("a q c -> q a c"),
+            )
+        load_w4(0)
+        load_x(1)
+        load_w8(0)
+        for q in range(4):
+            nc.sync.dma_start(
+                out=w8_plane[:].bitcast(I32)[32 * q : 32 * q + 16, :],
+                in_=w8s[:, 4 * q : 4 * q + 4, :],
+            )
+        load_x(2)
+        load_x(3)
+        nc.sync.dma_start(out=b_cols[:], in_=b.rearrange("(p c) -> p c", c=PACK))
+        load_w8(1)
+        load_x(4)
+        load_x(5)
+        load_w4(1)
+        load_w8(2)
+        for c in range(6, 10):
+            load_x(c)
+        load_w8(3)
+
+        def quant_a(c):
+            quantize(xa[c], xa_codes[c], xa_scales[c])
+
+        def quant_b(c):
+            quantize(xb[c], xb_codes[c], xb_scales[c])
+
+        for g in range(last):
+            c = 2 * g
+            relu_b(c)
+            relu_b(c + 1)
+            relu_a(c)
+            quant_a(c)
+            relu_a(c + 1)
+            quant_b(c)
+            quant_a(c + 1)
+            quant_b(c + 1)
+            mm_a(c)
+            mm_b(c)
+            mm_a(c + 1)
+            mm_b(c + 1)
+            if g == 1:
+                for j in range(PACK):
+                    nc.tensor.transpose(bias_ps[:, j, :], b_cols[:, j : j + 1].to_broadcast([P, P]), ident[:])
+            if g == 2:
+                nc.scalar.copy(out=bias[:].rearrange("m (p j) -> m p j", j=PACK), in_=bias_ps[:].rearrange("m j p -> m p j"))
+        first = 2 * last
+        for c in range(first, first + TILES):
+            relu_b(c)
+            relu_a(c)
+            if c > first:
+                quant_b(c - 1)
+            quant_a(c)
+            mm_a(c)
+        quant_b(first + TILES - 1)
+        for c in range(first, first + TILES):
+            mm_b(c)
+
+        pieces = [(i, 0, N) for i in range(TILES - 1)] + [(TILES - 1, 0, N // 2), (TILES - 1, N // 2, N // 2)]
+        for e, (i, n0, w) in enumerate(pieces):
+            pre = sb("pre%d" % e, [P, w], F32)
+            res = sb("res%d" % e, [P, w], F32)
+            nc.vector.tensor_tensor(out=pre[:], in0=acc[i][:, n0 : n0 + w], in1=bias[:, n0 : n0 + w], op=ALU.add)
+            nc.scalar.activation(out=res[:], in_=pre[:], func=ACT.Silu)
+            nc.sync.dma_start(out=out[i * T_TILE : (i + 1) * T_TILE, n0 : n0 + w], in_=res[:])

@@ -27,8 +27,9 @@ TILES = T // T_TILE
 def tile_mix_feat_tm_crelu_silu_kernel(tc, x, w4_words, w4_scales, w8_words, w8_scales, b, out):
     nc = tc.nc
     last = PASSES - 1
+    loads = [(g, 0, T) for g in range(last)] + [(last, 0, T - T_TILE), (last, T - T_TILE, T_TILE)]
     chunks = [(g, t0, 256) for g in range(last) for t0 in range(0, T, 256)]
-    chunks = chunks + [(last, t0, T_TILE) for t0 in range(0, T, T_TILE)]
+    chunks = chunks + [(last, 0, 256), (last, 256, T_TILE), (last, 384, T_TILE)]
 
     with ExitStack() as ctx:
         keep = ctx.enter_context(tc.tile_pool(name="keep", bufs=1))
@@ -38,7 +39,7 @@ def tile_mix_feat_tm_crelu_silu_kernel(tc, x, w4_words, w4_scales, w8_words, w8_
         def sb(name, shape, dtype):
             return keep.tile(shape, dtype, name=name, align_bytes=64)
 
-        raw = [sb("raw%d" % c, [P, PACK, w], F32) for c, (g, t0, w) in enumerate(chunks)]
+        raw = [sb("raw%d" % c, [P, PACK, w], F32) for c, (g, t0, w) in enumerate(loads)]
         xa = [sb("xa%d" % c, [P, w, PACK], BF16) for c, (g, t0, w) in enumerate(chunks)]
         xb = [sb("xb%d" % c, [P, w, PACK], BF16) for c, (g, t0, w) in enumerate(chunks)]
         xa_codes = [sb("xac%d" % c, [P, w], U32) for c, (g, t0, w) in enumerate(chunks)]
@@ -61,7 +62,7 @@ def tile_mix_feat_tm_crelu_silu_kernel(tc, x, w4_words, w4_scales, w8_words, w8_
         w8s = w8_scales.bitcast(I32)
 
         def load_x(c):
-            g, t0, w = chunks[c]
+            g, t0, w = loads[c]
             rows = x[g * K_PASS : (g + 1) * K_PASS, t0 : t0 + w]
             nc.sync.dma_start(out=raw[c][:], in_=rows.rearrange("(p j) t -> p j t", j=PACK))
 
@@ -78,9 +79,12 @@ def tile_mix_feat_tm_crelu_silu_kernel(tc, x, w4_words, w4_scales, w8_words, w8_
             )
 
         def views(c, dst):
+            g, t0, w = chunks[c]
+            src = [d for d, (lg, l0, lw) in enumerate(loads) if lg == g and l0 <= t0 < l0 + lw][0]
+            off = t0 - loads[src][1]
             return (
                 dst[c][:].rearrange("p (c i) j -> p c j i", i=4),
-                raw[c][:].rearrange("p j (c i) -> p c j i", i=4),
+                raw[src][:, :, off : off + w].rearrange("p j (c i) -> p c j i", i=4),
             )
 
         def relu_a(c):
@@ -129,6 +133,7 @@ def tile_mix_feat_tm_crelu_silu_kernel(tc, x, w4_words, w4_scales, w8_words, w8_
         make_identity(nc, ident[:])
 
         load_x(0)
+        nc.sync.dma_start(out=b_cols[:], in_=b.rearrange("(p c) -> p c", c=PACK))
         for r in range(4):
             nc.sync.dma_start(
                 out=w4_plane[:].bitcast(I32)[r:P:32, :, :],
@@ -136,22 +141,18 @@ def tile_mix_feat_tm_crelu_silu_kernel(tc, x, w4_words, w4_scales, w8_words, w8_
             )
         load_w4(0)
         load_x(1)
-        load_w8(0)
         for q in range(4):
             nc.sync.dma_start(
                 out=w8_plane[:].bitcast(I32)[32 * q : 32 * q + 16, :],
                 in_=w8s[:, 4 * q : 4 * q + 4, :],
             )
+        load_w8(0)
         load_x(2)
-        load_x(3)
-        nc.sync.dma_start(out=b_cols[:], in_=b.rearrange("(p c) -> p c", c=PACK))
         load_w8(1)
-        load_x(4)
-        load_x(5)
         load_w4(1)
+        load_x(3)
         load_w8(2)
-        for c in range(6, 10):
-            load_x(c)
+        load_x(4)
         load_w8(3)
 
         def quant_a(c):
@@ -160,36 +161,35 @@ def tile_mix_feat_tm_crelu_silu_kernel(tc, x, w4_words, w4_scales, w8_words, w8_
         def quant_b(c):
             quantize(xb[c], xb_codes[c], xb_scales[c])
 
-        for g in range(last):
+        for j in range(PACK):
+            nc.tensor.transpose(bias_ps[:, j, :], b_cols[:, j : j + 1].to_broadcast([P, P]), ident[:])
+        for g in range(PASSES):
             c = 2 * g
             relu_b(c)
             relu_b(c + 1)
             relu_a(c)
-            quant_a(c)
             relu_a(c + 1)
-            quant_b(c)
-            quant_a(c + 1)
-            quant_b(c + 1)
-            mm_a(c)
-            mm_b(c)
-            mm_a(c + 1)
-            mm_b(c + 1)
-            if g == 1:
-                for j in range(PACK):
-                    nc.tensor.transpose(bias_ps[:, j, :], b_cols[:, j : j + 1].to_broadcast([P, P]), ident[:])
-            if g == 2:
-                nc.scalar.copy(out=bias[:].rearrange("m (p j) -> m p j", j=PACK), in_=bias_ps[:].rearrange("m j p -> m p j"))
-        first = 2 * last
-        for c in range(first, first + TILES):
-            relu_b(c)
-            relu_a(c)
-            if c > first:
-                quant_b(c - 1)
             quant_a(c)
+            quant_a(c + 1)
+            quant_b(c)
             mm_a(c)
-        quant_b(first + TILES - 1)
-        for c in range(first, first + TILES):
-            mm_b(c)
+            mm_a(c + 1)
+            if g == 0:
+                nc.scalar.copy(out=bias[:].rearrange("m (p j) -> m p j", j=PACK), in_=bias_ps[:].rearrange("m j p -> m p j"))
+            if g < last:
+                quant_b(c + 1)
+                mm_b(c)
+                mm_b(c + 1)
+        c = 2 * last
+        relu_b(c + 2)
+        relu_a(c + 2)
+        quant_b(c + 1)
+        quant_a(c + 2)
+        quant_b(c + 2)
+        mm_b(c)
+        mm_b(c + 1)
+        mm_a(c + 2)
+        mm_b(c + 2)
 
         pieces = [(i, 0, N) for i in range(TILES - 1)] + [(TILES - 1, 0, N // 2), (TILES - 1, N // 2, N // 2)]
         for e, (i, n0, w) in enumerate(pieces):

@@ -27,7 +27,7 @@ TILES = T // T_TILE
 def tile_mix_feat_tm_crelu_silu_kernel(tc, x, w4_words, w4_scales, w8_words, w8_scales, b, out):
     nc = tc.nc
     last = PASSES - 1
-    loads = [(g, 0, T) for g in range(last)] + [(last, 0, T - T_TILE), (last, T - T_TILE, T_TILE)]
+    loads = [(g, 0, T) for g in range(last)] + [(last, 0, 256), (last, 256, T_TILE), (last, 384, T_TILE)]
     chunks = [(g, t0, 256) for g in range(last) for t0 in range(0, T, 256)]
     chunks = chunks + [(last, 0, 256), (last, 256, T_TILE), (last, 384, T_TILE)]
 
@@ -153,6 +153,7 @@ def tile_mix_feat_tm_crelu_silu_kernel(tc, x, w4_words, w4_scales, w8_words, w8_
         load_x(3)
         load_w8(2)
         load_x(4)
+        load_x(5)
         load_w8(3)
 
         def quant_a(c):
@@ -163,7 +164,7 @@ def tile_mix_feat_tm_crelu_silu_kernel(tc, x, w4_words, w4_scales, w8_words, w8_
 
         for j in range(PACK):
             nc.tensor.transpose(bias_ps[:, j, :], b_cols[:, j : j + 1].to_broadcast([P, P]), ident[:])
-        for g in range(PASSES):
+        for g in range(last):
             c = 2 * g
             relu_b(c)
             relu_b(c + 1)
@@ -176,25 +177,35 @@ def tile_mix_feat_tm_crelu_silu_kernel(tc, x, w4_words, w4_scales, w8_words, w8_
             mm_a(c + 1)
             if g == 0:
                 nc.scalar.copy(out=bias[:].rearrange("m (p j) -> m p j", j=PACK), in_=bias_ps[:].rearrange("m j p -> m p j"))
-            if g < last:
+            if g < last - 1:
                 quant_b(c + 1)
                 mm_b(c)
                 mm_b(c + 1)
         c = 2 * last
-        relu_b(c + 2)
-        relu_a(c + 2)
-        quant_b(c + 1)
-        quant_a(c + 2)
+        for d in range(c, c + 3):
+            relu_b(d)
+            relu_a(d)
+            quant_b(d - 1)
+            quant_a(d)
         quant_b(c + 2)
+        mm_b(c - 2)
+        mm_b(c - 1)
+        mm_a(c)
+        mm_a(c + 1)
         mm_b(c)
-        mm_b(c + 1)
         mm_a(c + 2)
+        mm_b(c + 1)
         mm_b(c + 2)
 
-        pieces = [(i, 0, N) for i in range(TILES - 1)] + [(TILES - 1, 0, N // 2), (TILES - 1, N // 2, N // 2)]
-        for e, (i, n0, w) in enumerate(pieces):
-            pre = sb("pre%d" % e, [P, w], F32)
-            res = sb("res%d" % e, [P, w], F32)
-            nc.vector.tensor_tensor(out=pre[:], in0=acc[i][:, n0 : n0 + w], in1=bias[:, n0 : n0 + w], op=ALU.add)
-            nc.scalar.activation(out=res[:], in_=pre[:], func=ACT.Silu)
-            nc.sync.dma_start(out=out[i * T_TILE : (i + 1) * T_TILE, n0 : n0 + w], in_=res[:])
+        half = N // 2
+        for i in range(TILES):
+            res = sb("res%d" % i, [P, N], F32)
+            rows = slice(i * T_TILE, (i + 1) * T_TILE)
+            for n0 in (0, half):
+                pre = sb("pre%d_%d" % (i, n0), [P, half], F32)
+                nc.vector.tensor_tensor(out=pre[:], in0=acc[i][:, n0 : n0 + half], in1=bias[:, n0 : n0 + half], op=ALU.add)
+                nc.scalar.activation(out=res[:, n0 : n0 + half], in_=pre[:], func=ACT.Silu)
+                if i in (0, TILES - 1):
+                    nc.sync.dma_start(out=out[rows, n0 : n0 + half], in_=res[:, n0 : n0 + half])
+            if i not in (0, TILES - 1):
+                nc.sync.dma_start(out=out[rows, :], in_=res[:])

@@ -130,10 +130,15 @@ def tile_mix_feat_tm_crelu_silu_kernel(tc, x, w4_words, w4_scales, w8_words, w8_
         nc.vector.memset(w8_plane[:].bitcast(I32), 0)
         nc.vector.memset(zero_in[:], 0.0)
         nc.scalar.activation(out=zero[:], in_=zero_in[:], func=ACT.Silu)
+        nc.gpsimd.dma_start(out=b_cols[:], in_=b.rearrange("(p c) -> p c", c=PACK))
         make_identity(nc, ident[:])
+        for q in range(4):
+            nc.gpsimd.dma_start(
+                out=w8_plane[:].bitcast(I32)[32 * q : 32 * q + 16, :],
+                in_=w8s[:, 4 * q : 4 * q + 4, :],
+            )
 
         load_x(0)
-        nc.sync.dma_start(out=b_cols[:], in_=b.rearrange("(p c) -> p c", c=PACK))
         for r in range(4):
             nc.sync.dma_start(
                 out=w4_plane[:].bitcast(I32)[r:P:32, :, :],
@@ -141,11 +146,6 @@ def tile_mix_feat_tm_crelu_silu_kernel(tc, x, w4_words, w4_scales, w8_words, w8_
             )
         load_w4(0)
         load_x(1)
-        for q in range(4):
-            nc.sync.dma_start(
-                out=w8_plane[:].bitcast(I32)[32 * q : 32 * q + 16, :],
-                in_=w8s[:, 4 * q : 4 * q + 4, :],
-            )
         load_w8(0)
         load_x(2)
         load_w8(1)
@@ -190,12 +190,9 @@ def tile_mix_feat_tm_crelu_silu_kernel(tc, x, w4_words, w4_scales, w8_words, w8_
         quant_b(c + 2)
         mm_b(c - 2)
         mm_b(c - 1)
-        mm_a(c)
-        mm_a(c + 1)
-        mm_b(c)
-        mm_a(c + 2)
-        mm_b(c + 1)
-        mm_b(c + 2)
+        for d in range(c, c + 3):
+            mm_a(d)
+            mm_b(d)
 
         half = N // 2
         for i in range(TILES):

@@ -20,16 +20,24 @@ P = 128
 PACK = 4
 K_PASS = P * PACK
 PASSES = K // K_PASS
+LAST = PASSES - 1
 T_TILE = 128
 TILES = T // T_TILE
+QUADRANT = 32
+QUADRANTS = P // QUADRANT
+SCALE_ROWS = 4
+LINE = 4
+B_COLS = N // P
+T_HALF = T // 2
+N_HALF = N // 2
+
+LAST_CHUNKS = [(LAST, 0, T_HALF), (LAST, T_HALF, T_TILE), (LAST, T - T_TILE, T_TILE)]
+CHUNKS = [(g, t0, T_HALF) for g in range(LAST) for t0 in (0, T_HALF)] + LAST_CHUNKS
+X_LOADS = [(g, 0, T) for g in range(LAST)] + LAST_CHUNKS
 
 
 def tile_mix_feat_tm_crelu_silu_kernel(tc, x, w4_words, w4_scales, w8_words, w8_scales, b, out):
     nc = tc.nc
-    last = PASSES - 1
-    loads = [(g, 0, T) for g in range(last)] + [(last, 0, 256), (last, 256, T_TILE), (last, 384, T_TILE)]
-    chunks = [(g, t0, 256) for g in range(last) for t0 in range(0, T, 256)]
-    chunks = chunks + [(last, 0, 256), (last, 256, T_TILE), (last, 384, T_TILE)]
 
     with ExitStack() as ctx:
         keep = ctx.enter_context(tc.tile_pool(name="keep", bufs=1))
@@ -39,37 +47,34 @@ def tile_mix_feat_tm_crelu_silu_kernel(tc, x, w4_words, w4_scales, w8_words, w8_
         def sb(name, shape, dtype):
             return keep.tile(shape, dtype, name=name, align_bytes=64)
 
-        raw = [sb("raw%d" % c, [P, PACK, w], F32) for c, (g, t0, w) in enumerate(loads)]
-        xa = [sb("xa%d" % c, [P, w, PACK], BF16) for c, (g, t0, w) in enumerate(chunks)]
-        xb = [sb("xb%d" % c, [P, w, PACK], BF16) for c, (g, t0, w) in enumerate(chunks)]
-        xa_codes = [sb("xac%d" % c, [P, w], U32) for c, (g, t0, w) in enumerate(chunks)]
-        xb_codes = [sb("xbc%d" % c, [P, w], U32) for c, (g, t0, w) in enumerate(chunks)]
-        xa_scales = [sb("xas%d" % c, [P, w], U8) for c, (g, t0, w) in enumerate(chunks)]
-        xb_scales = [sb("xbs%d" % c, [P, w], U8) for c, (g, t0, w) in enumerate(chunks)]
-        w4 = [sb("w4_%d" % h, [P, 2, 2 * N], U8) for h in range(PASSES // 2)]
+        raw = [sb("raw%d" % d, [P, PACK, width], F32) for d, (g, t0, width) in enumerate(X_LOADS)]
+        xa = [sb("xa%d" % c, [P, width, PACK], BF16) for c, (g, t0, width) in enumerate(CHUNKS)]
+        xb = [sb("xb%d" % c, [P, width, PACK], BF16) for c, (g, t0, width) in enumerate(CHUNKS)]
+        xa_codes = [sb("xac%d" % c, [P, width], U32) for c, (g, t0, width) in enumerate(CHUNKS)]
+        xb_codes = [sb("xbc%d" % c, [P, width], U32) for c, (g, t0, width) in enumerate(CHUNKS)]
+        xa_scales = [sb("xas%d" % c, [P, width], U8) for c, (g, t0, width) in enumerate(CHUNKS)]
+        xb_scales = [sb("xbs%d" % c, [P, width], U8) for c, (g, t0, width) in enumerate(CHUNKS)]
+        w4 = [sb("w4_%d" % pair, [P, 2, 2 * N], U8) for pair in range(PASSES // 2)]
         w8 = [sb("w8_%d" % g, [P, N], U32) for g in range(PASSES)]
-        w4_plane = sb("w4_plane", [P, PASSES, N], U8)
-        w8_plane = sb("w8_plane", [P, N], U8)
+        w4_scale_tile = sb("w4_plane", [P, PASSES, N], U8)
+        w8_scale_tile = sb("w8_plane", [P, N], U8)
         ident = sb("ident", [P, P], F32)
-        b_cols = sb("b_cols", [P, PACK], F32)
+        b_cols = sb("b_cols", [P, B_COLS], F32)
         bias = sb("bias", [P, N], F32)
         zero_in = sb("zero_in", [P, 1], F32)
         zero = sb("zero", [P, 1], F32)
         acc = [psum.tile([P, N], F32, name="acc%d" % i) for i in range(TILES)]
-        bias_ps = psum.tile([P, PACK, P], F32, name="bias_ps")
+        bias_ps = psum.tile([P, B_COLS, P], F32, name="bias_ps")
 
-        w4s = w4_scales.bitcast(I32)
-        w8s = w8_scales.bitcast(I32)
+        def load_x(d):
+            g, t0, width = X_LOADS[d]
+            rows = x[g * K_PASS : (g + 1) * K_PASS, t0 : t0 + width]
+            nc.sync.dma_start(out=raw[d][:], in_=rows.rearrange("(p j) t -> p j t", j=PACK))
 
-        def load_x(c):
-            g, t0, w = loads[c]
-            rows = x[g * K_PASS : (g + 1) * K_PASS, t0 : t0 + w]
-            nc.sync.dma_start(out=raw[c][:], in_=rows.rearrange("(p j) t -> p j t", j=PACK))
-
-        def load_w4(h):
+        def load_w4(pair):
             nc.sync.dma_start(
-                out=w4[h][:].bitcast(I32),
-                in_=w4_words[2 * h : 2 * h + 2].bitcast(I32).rearrange("a p c -> p a c"),
+                out=w4[pair][:].bitcast(I32),
+                in_=w4_words[2 * pair : 2 * pair + 2].bitcast(I32).rearrange("a p c -> p a c"),
             )
 
         def load_w8(g):
@@ -78,21 +83,38 @@ def tile_mix_feat_tm_crelu_silu_kernel(tc, x, w4_words, w4_scales, w8_words, w8_
                 in_=w8_words[g].rearrange("p n i -> p (n i)").bitcast(I32),
             )
 
-        def views(c, dst):
-            g, t0, w = chunks[c]
-            src = [d for d, (lg, l0, lw) in enumerate(loads) if lg == g and l0 <= t0 < l0 + lw][0]
-            off = t0 - loads[src][1]
+        def load_w4_scales():
+            rows = w4_scales.bitcast(I32)
+            for r in range(SCALE_ROWS):
+                nc.sync.dma_start(
+                    out=w4_scale_tile[:].bitcast(I32)[r:P:QUADRANT, :, :],
+                    in_=rows[:, r : QUADRANTS * SCALE_ROWS : SCALE_ROWS, :].rearrange("a q c -> q a c"),
+                )
+
+        def load_w8_scales():
+            rows = w8_scales.bitcast(I32)
+            for quad in range(QUADRANTS):
+                first = QUADRANT * quad
+                nc.sync.dma_start(
+                    out=w8_scale_tile[:].bitcast(I32)[first : first + PASSES * SCALE_ROWS, :],
+                    in_=rows[:, SCALE_ROWS * quad : SCALE_ROWS * (quad + 1), :],
+                )
+
+        def interleaving_views(c, values):
+            g, t0, width = CHUNKS[c]
+            d = [e for e, (lg, l0, lw) in enumerate(X_LOADS) if lg == g and l0 <= t0 < l0 + lw][0]
+            off = t0 - X_LOADS[d][1]
             return (
-                dst[c][:].rearrange("p (c i) j -> p c j i", i=4),
-                raw[src][:, :, off : off + w].rearrange("p j (c i) -> p c j i", i=4),
+                values[c][:].rearrange("p (s i) j -> p s j i", i=LINE),
+                raw[d][:, :, off : off + width].rearrange("p j (s i) -> p s j i", i=LINE),
             )
 
         def relu_a(c):
-            dst, src = views(c, xa)
+            dst, src = interleaving_views(c, xa)
             nc.vector.tensor_scalar(out=dst, in0=src, scalar1=0.0, scalar2=None, op0=ALU.max)
 
         def relu_b(c):
-            dst, src = views(c, xb)
+            dst, src = interleaving_views(c, xb)
             nc.scalar.activation(out=dst, in_=src, func=ACT.Relu, bias=zero[:], scale=-1.0)
 
         def quantize(values, codes, scales):
@@ -100,109 +122,106 @@ def tile_mix_feat_tm_crelu_silu_kernel(tc, x, w4_words, w4_scales, w8_words, w8_
                 out=codes[:].bitcast(FP8X4), scales=scales[:], in_=values[:].rearrange("p t j -> p (t j)")
             )
 
-        def mm_a(c):
-            g, t0, w = chunks[c]
-            for s in range(0, w, T_TILE):
+        def quantize_a(c):
+            quantize(xa[c], xa_codes[c], xa_scales[c])
+
+        def quantize_b(c):
+            quantize(xb[c], xb_codes[c], xb_scales[c])
+
+        def matmul_a(c):
+            g, t0, width = CHUNKS[c]
+            for s0 in range(0, width, T_TILE):
                 nc.tensor.matmul_mx(
-                    out=acc[(t0 + s) // T_TILE][:],
-                    lhsT=xa_codes[c][:, s : s + T_TILE].bitcast(FP8X4),
-                    lhsT_scale=xa_scales[c][:, s : s + T_TILE],
+                    out=acc[(t0 + s0) // T_TILE][:],
+                    lhsT=xa_codes[c][:, s0 : s0 + T_TILE].bitcast(FP8X4),
+                    lhsT_scale=xa_scales[c][:, s0 : s0 + T_TILE],
                     rhs=w4[g // 2][:, g % 2, :].bitcast(FP4X4),
-                    rhs_scale=w4_plane[:, g, :],
+                    rhs_scale=w4_scale_tile[:, g, :],
                     start=(g == 0),
                     stop=False,
                 )
 
-        def mm_b(c):
-            g, t0, w = chunks[c]
-            for s in range(0, w, T_TILE):
+        def matmul_b(c):
+            g, t0, width = CHUNKS[c]
+            for s0 in range(0, width, T_TILE):
                 nc.tensor.matmul_mx(
-                    out=acc[(t0 + s) // T_TILE][:],
-                    lhsT=xb_codes[c][:, s : s + T_TILE].bitcast(FP8X4),
-                    lhsT_scale=xb_scales[c][:, s : s + T_TILE],
+                    out=acc[(t0 + s0) // T_TILE][:],
+                    lhsT=xb_codes[c][:, s0 : s0 + T_TILE].bitcast(FP8X4),
+                    lhsT_scale=xb_scales[c][:, s0 : s0 + T_TILE],
                     rhs=w8[g][:].bitcast(FP8X4),
-                    rhs_scale=w8_plane[PACK * g :, :],
+                    rhs_scale=w8_scale_tile[SCALE_ROWS * g :, :],
                     start=False,
-                    stop=(g == last),
+                    stop=(g == LAST),
                 )
 
-        nc.vector.memset(w4_plane[:].bitcast(I32), 0)
-        nc.vector.memset(w8_plane[:].bitcast(I32), 0)
+        nc.vector.memset(w4_scale_tile[:].bitcast(I32), 0)
+        nc.vector.memset(w8_scale_tile[:].bitcast(I32), 0)
         nc.vector.memset(zero_in[:], 0.0)
         nc.scalar.activation(out=zero[:], in_=zero_in[:], func=ACT.Silu)
-        nc.gpsimd.dma_start(out=b_cols[:], in_=b.rearrange("(p c) -> p c", c=PACK))
         make_identity(nc, ident[:])
-        for q in range(4):
-            nc.gpsimd.dma_start(
-                out=w8_plane[:].bitcast(I32)[32 * q : 32 * q + 16, :],
-                in_=w8s[:, 4 * q : 4 * q + 4, :],
-            )
 
         load_x(0)
-        for r in range(4):
-            nc.sync.dma_start(
-                out=w4_plane[:].bitcast(I32)[r:P:32, :, :],
-                in_=w4s[:, r:16:4, :].rearrange("a q c -> q a c"),
-            )
+        nc.sync.dma_start(out=b_cols[:], in_=b.rearrange("(p j) -> p j", j=B_COLS))
+        load_w4_scales()
         load_w4(0)
         load_x(1)
+        load_w8_scales()
         load_w8(0)
         load_x(2)
         load_w8(1)
         load_w4(1)
-        load_x(3)
+        load_x(LAST)
         load_w8(2)
-        load_x(4)
-        load_x(5)
-        load_w8(3)
+        load_x(LAST + 1)
+        load_x(LAST + 2)
+        load_w8(LAST)
 
-        def quant_a(c):
-            quantize(xa[c], xa_codes[c], xa_scales[c])
-
-        def quant_b(c):
-            quantize(xb[c], xb_codes[c], xb_scales[c])
-
-        for j in range(PACK):
+        for j in range(B_COLS):
             nc.tensor.transpose(bias_ps[:, j, :], b_cols[:, j : j + 1].to_broadcast([P, P]), ident[:])
-        for g in range(last):
+
+        for g in range(LAST):
             c = 2 * g
             relu_b(c)
             relu_b(c + 1)
             relu_a(c)
             relu_a(c + 1)
-            quant_a(c)
-            quant_a(c + 1)
-            quant_b(c)
-            mm_a(c)
-            mm_a(c + 1)
+            quantize_a(c)
+            quantize_a(c + 1)
+            quantize_b(c)
+            matmul_a(c)
+            matmul_a(c + 1)
             if g == 0:
-                nc.scalar.copy(out=bias[:].rearrange("m (p j) -> m p j", j=PACK), in_=bias_ps[:].rearrange("m j p -> m p j"))
-            if g < last - 1:
-                quant_b(c + 1)
-                mm_b(c)
-                mm_b(c + 1)
-        c = 2 * last
-        for d in range(c, c + 3):
-            relu_b(d)
-            relu_a(d)
-            quant_b(d - 1)
-            quant_a(d)
-        quant_b(c + 2)
-        mm_b(c - 2)
-        mm_b(c - 1)
-        for d in range(c, c + 3):
-            mm_a(d)
-            mm_b(d)
+                nc.scalar.copy(
+                    out=bias[:].rearrange("m (p j) -> m p j", j=B_COLS), in_=bias_ps[:].rearrange("m j p -> m p j")
+                )
+            if g < LAST - 1:
+                quantize_b(c + 1)
+                matmul_b(c)
+                matmul_b(c + 1)
 
-        half = N // 2
+        last_chunks = range(2 * LAST, len(CHUNKS))
+        for c in last_chunks:
+            relu_b(c)
+            relu_a(c)
+            quantize_b(c - 1)
+            quantize_a(c)
+        quantize_b(len(CHUNKS) - 1)
+        matmul_b(2 * LAST - 2)
+        matmul_b(2 * LAST - 1)
+        for c in last_chunks:
+            matmul_a(c)
+            matmul_b(c)
+
         for i in range(TILES):
             res = sb("res%d" % i, [P, N], F32)
             rows = slice(i * T_TILE, (i + 1) * T_TILE)
-            for n0 in (0, half):
-                pre = sb("pre%d_%d" % (i, n0), [P, half], F32)
-                nc.vector.tensor_tensor(out=pre[:], in0=acc[i][:, n0 : n0 + half], in1=bias[:, n0 : n0 + half], op=ALU.add)
-                nc.scalar.activation(out=res[:, n0 : n0 + half], in_=pre[:], func=ACT.Silu)
-                if i in (0, TILES - 1):
-                    nc.sync.dma_start(out=out[rows, n0 : n0 + half], in_=res[:, n0 : n0 + half])
-            if i not in (0, TILES - 1):
+            store_halves = i in (0, TILES - 1)
+            for n0 in (0, N_HALF):
+                cols = slice(n0, n0 + N_HALF)
+                pre = sb("pre%d_%d" % (i, n0), [P, N_HALF], F32)
+                nc.vector.tensor_tensor(out=pre[:], in0=acc[i][:, cols], in1=bias[:, cols], op=ALU.add)
+                nc.scalar.activation(out=res[:, cols], in_=pre[:], func=ACT.Silu)
+                if store_halves:
+                    nc.sync.dma_start(out=out[rows, cols], in_=res[:, cols])
+            if not store_halves:
                 nc.sync.dma_start(out=out[rows, :], in_=res[:])

from contextlib import ExitStack

import concourse.mybir as mybir
from concourse.masks import make_identity

K, N, T = 2048, 512, 512
FLOPS = 2 * 2 * K * N * T

F32 = mybir.dt.float32
BF16 = mybir.dt.bfloat16
I32 = mybir.dt.int32
U32 = mybir.dt.uint32
U8 = mybir.dt.uint8
FP8X4 = mybir.dt.float8_e4m3fn_x4
FP4X4 = mybir.dt.float4_e2m1fn_x4
ACT = mybir.ActivationFunctionType
ALU = mybir.AluOpType

P = 128
PACK = 4
K_PASS = P * PACK
PASSES = K // K_PASS
LAST = PASSES - 1
T_TILE = 128
TILES = T // T_TILE
QUADRANT = 32
QUADRANTS = P // QUADRANT
SCALE_ROWS = 4
LINE = 4
B_COLS = N // P
T_HALF = T // 2
N_HALF = N // 2

LAST_CHUNKS = [(LAST, 0, T_HALF), (LAST, T_HALF, T_TILE), (LAST, T - T_TILE, T_TILE)]
CHUNKS = [(g, t0, T_HALF) for g in range(LAST) for t0 in (0, T_HALF)] + LAST_CHUNKS
X_LOADS = [(g, 0, T) for g in range(LAST)] + LAST_CHUNKS


def tile_mix_feat_tm_crelu_silu_kernel(tc, x, w4_words, w4_scales, w8_words, w8_scales, b, out):
    nc = tc.nc

    with ExitStack() as ctx:
        keep = ctx.enter_context(tc.tile_pool(name="keep", bufs=1))
        psum = ctx.enter_context(tc.psum_pool(name="psum", bufs=1))
        ctx.enter_context(tc.manual_schedule())

        def sb(name, shape, dtype):
            return keep.tile(shape, dtype, name=name, align_bytes=64)

        raw = [sb("raw%d" % d, [P, PACK, width], F32) for d, (g, t0, width) in enumerate(X_LOADS)]
        xa = [sb("xa%d" % c, [P, width, PACK], BF16) for c, (g, t0, width) in enumerate(CHUNKS)]
        xb = [sb("xb%d" % c, [P, width, PACK], BF16) for c, (g, t0, width) in enumerate(CHUNKS)]
        xa_codes = [sb("xac%d" % c, [P, width], U32) for c, (g, t0, width) in enumerate(CHUNKS)]
        xb_codes = [sb("xbc%d" % c, [P, width], U32) for c, (g, t0, width) in enumerate(CHUNKS)]
        xa_scales = [sb("xas%d" % c, [P, width], U8) for c, (g, t0, width) in enumerate(CHUNKS)]
        xb_scales = [sb("xbs%d" % c, [P, width], U8) for c, (g, t0, width) in enumerate(CHUNKS)]
        w4 = [sb("w4_%d" % pair, [P, 2, 2 * N], U8) for pair in range(PASSES // 2)]
        w8 = [sb("w8_%d" % g, [P, N], U32) for g in range(PASSES)]
        w4_scale_tile = sb("w4_plane", [P, PASSES, N], U8)
        w8_scale_tile = sb("w8_plane", [P, N], U8)
        ident = sb("ident", [P, P], F32)
        b_cols = sb("b_cols", [P, B_COLS], F32)
        bias = sb("bias", [P, N], F32)
        zero_in = sb("zero_in", [P, 1], F32)
        zero = sb("zero", [P, 1], F32)
        acc = [psum.tile([P, N], F32, name="acc%d" % i) for i in range(TILES)]
        bias_ps = psum.tile([P, B_COLS, P], F32, name="bias_ps")

        def load_x(d):
            g, t0, width = X_LOADS[d]
            rows = x[g * K_PASS : (g + 1) * K_PASS, t0 : t0 + width]
            nc.sync.dma_start(out=raw[d][:], in_=rows.rearrange("(p j) t -> p j t", j=PACK))

        def load_w4(pair):
            nc.sync.dma_start(
                out=w4[pair][:].bitcast(I32),
                in_=w4_words[2 * pair : 2 * pair + 2].bitcast(I32).rearrange("a p c -> p a c"),
            )

        def load_w8(g):
            nc.sync.dma_start(
                out=w8[g][:].bitcast(I32),
                in_=w8_words[g].rearrange("p n i -> p (n i)").bitcast(I32),
            )

        def load_w4_scales():
            rows = w4_scales.bitcast(I32)
            for r in range(SCALE_ROWS):
                nc.sync.dma_start(
                    out=w4_scale_tile[:].bitcast(I32)[r:P:QUADRANT, :, :],
                    in_=rows[:, r : QUADRANTS * SCALE_ROWS : SCALE_ROWS, :].rearrange("a q c -> q a c"),
                )

        def load_w8_scales():
            rows = w8_scales.bitcast(I32)
            for quad in range(QUADRANTS):
                first = QUADRANT * quad
                nc.sync.dma_start(
                    out=w8_scale_tile[:].bitcast(I32)[first : first + PASSES * SCALE_ROWS, :],
                    in_=rows[:, SCALE_ROWS * quad : SCALE_ROWS * (quad + 1), :],
                )

        def interleaving_views(c, values):
            g, t0, width = CHUNKS[c]
            d = [e for e, (lg, l0, lw) in enumerate(X_LOADS) if lg == g and l0 <= t0 < l0 + lw][0]
            off = t0 - X_LOADS[d][1]
            return (
                values[c][:].rearrange("p (s i) j -> p s j i", i=LINE),
                raw[d][:, :, off : off + width].rearrange("p j (s i) -> p s j i", i=LINE),
            )

        def relu_a(c):
            dst, src = interleaving_views(c, xa)
            nc.vector.tensor_scalar(out=dst, in0=src, scalar1=0.0, scalar2=None, op0=ALU.max)

        def relu_b(c):
            dst, src = interleaving_views(c, xb)
            nc.scalar.activation(out=dst, in_=src, func=ACT.Relu, bias=zero[:], scale=-1.0)

        def quantize(values, codes, scales):
            nc.vector.quantize_mx(
                out=codes[:].bitcast(FP8X4), scales=scales[:], in_=values[:].rearrange("p t j -> p (t j)")
            )

        def quantize_a(c):
            quantize(xa[c], xa_codes[c], xa_scales[c])

        def quantize_b(c):
            quantize(xb[c], xb_codes[c], xb_scales[c])

        def matmul_a(c):
            g, t0, width = CHUNKS[c]
            for s0 in range(0, width, T_TILE):
                nc.tensor.matmul_mx(
                    out=acc[(t0 + s0) // T_TILE][:],
                    lhsT=xa_codes[c][:, s0 : s0 + T_TILE].bitcast(FP8X4),
                    lhsT_scale=xa_scales[c][:, s0 : s0 + T_TILE],
                    rhs=w4[g // 2][:, g % 2, :].bitcast(FP4X4),
                    rhs_scale=w4_scale_tile[:, g, :],
                    start=(g == 0),
                    stop=False,
                )

        def matmul_b(c):
            g, t0, width = CHUNKS[c]
            for s0 in range(0, width, T_TILE):
                nc.tensor.matmul_mx(
                    out=acc[(t0 + s0) // T_TILE][:],
                    lhsT=xb_codes[c][:, s0 : s0 + T_TILE].bitcast(FP8X4),
                    lhsT_scale=xb_scales[c][:, s0 : s0 + T_TILE],
                    rhs=w8[g][:].bitcast(FP8X4),
                    rhs_scale=w8_scale_tile[SCALE_ROWS * g :, :],
                    start=False,
                    stop=(g == LAST),
                )

        nc.vector.memset(w4_scale_tile[:].bitcast(I32), 0)
        nc.vector.memset(w8_scale_tile[:].bitcast(I32), 0)
        nc.vector.memset(zero_in[:], 0.0)
        nc.scalar.activation(out=zero[:], in_=zero_in[:], func=ACT.Silu)
        make_identity(nc, ident[:])

        load_x(0)
        nc.sync.dma_start(out=b_cols[:], in_=b.rearrange("(p j) -> p j", j=B_COLS))
        load_w4_scales()
        load_w4(0)
        load_x(1)
        load_w8_scales()
        load_w8(0)
        load_x(2)
        load_w8(1)
        load_w4(1)
        load_x(LAST)
        load_w8(2)
        load_x(LAST + 1)
        load_x(LAST + 2)
        load_w8(LAST)

        for j in range(B_COLS):
            nc.tensor.transpose(bias_ps[:, j, :], b_cols[:, j : j + 1].to_broadcast([P, P]), ident[:])

        for g in range(LAST):
            c = 2 * g
            relu_b(c)
            relu_b(c + 1)
            relu_a(c)
            relu_a(c + 1)
            quantize_a(c)
            quantize_a(c + 1)
            quantize_b(c)
            matmul_a(c)
            matmul_a(c + 1)
            if g == 0:
                nc.scalar.copy(
                    out=bias[:].rearrange("m (p j) -> m p j", j=B_COLS), in_=bias_ps[:].rearrange("m j p -> m p j")
                )
            if g < LAST - 1:
                quantize_b(c + 1)
                matmul_b(c)
                matmul_b(c + 1)

        last_chunks = range(2 * LAST, len(CHUNKS))
        for c in last_chunks:
            relu_b(c)
            relu_a(c)
            quantize_b(c - 1)
            quantize_a(c)
        quantize_b(len(CHUNKS) - 1)
        matmul_b(2 * LAST - 2)
        matmul_b(2 * LAST - 1)
        for c in last_chunks:
            matmul_a(c)
            matmul_b(c)

        for i in range(TILES):
            res = sb("res%d" % i, [P, N], F32)
            rows = slice(i * T_TILE, (i + 1) * T_TILE)
            store_halves = i in (0, TILES - 1)
            for n0 in (0, N_HALF):
                cols = slice(n0, n0 + N_HALF)
                pre = sb("pre%d_%d" % (i, n0), [P, N_HALF], F32)
                nc.vector.tensor_tensor(out=pre[:], in0=acc[i][:, cols], in1=bias[:, cols], op=ALU.add)
                nc.scalar.activation(out=res[:, cols], in_=pre[:], func=ACT.Silu)
                if store_halves:
                    nc.sync.dma_start(out=out[rows, cols], in_=res[:, cols])
            if not store_halves:
                nc.sync.dma_start(out=out[rows, :], in_=res[:])
